import numpy as np
import ml_dtypes


def mxq(x, axis, fmt="e4m3"):
    dtype, down = {"e4m3": (ml_dtypes.float8_e4m3fn, 7), "e5m2": (ml_dtypes.float8_e5m2, 14)}[fmt]
    v = np.moveaxis(np.asarray(x, np.float32).astype(ml_dtypes.bfloat16).astype(np.float64), axis, -1)
    blocks = v.reshape(v.shape[:-1] + (-1, 32))
    amax = np.abs(blocks).max(-1, keepdims=True)
    byte = np.maximum(np.where(amax > 0, np.frexp(amax)[1] - 1 + 127, 0) - down, 1)
    scale = np.exp2(byte - 127.0)
    codes = (blocks / scale).astype(np.float32).astype(dtype).astype(np.float64)
    return np.moveaxis((codes * scale).reshape(v.shape), -1, axis)


WIDE = False


def mx_kscale(k):
    if not WIDE:
        return np.ones(k)
    levels = np.array([10, -10, 5, -5, 0])
    if k % 512:
        return np.exp2(np.random.permutation(np.resize(levels, k // 32))).repeat(32)
    a = np.empty((k // 512, 16))
    for p in range(k // 512):
        a[p, :8] = np.random.permutation(np.resize(levels, 8))
        for g in range(8):
            far = levels[np.abs(levels - a[p, g]) >= 10]
            a[p, g + 8] = far[np.random.randint(len(far))]
    return np.exp2(a.ravel()).repeat(32)


def f64(x):
    return np.asarray(x).astype(np.float64)


def striped(idx):
    return np.tile(np.asarray(idx).reshape(-1, 16).T, (8, 1)).astype(np.uint16)


def unstriped(offs):
    return offs[:16].T.reshape(-1).astype(np.int64)


E2M1 = np.array([0.0, 0.5, 1.0, 1.5, 2.0, 3.0, 4.0, 6.0, -0.0, -0.5, -1.0, -1.5, -2.0, -3.0, -4.0, -6.0])


def pack_weight(w, fmt):
    k, n = w.shape
    w = f64(np.asarray(w, np.float32).astype(ml_dtypes.bfloat16)).reshape(k // 32, 32, n)
    amax = np.abs(w).max(1)
    if fmt == "e4m3":
        byte = np.frexp(amax)[1] - 1 + 127 - 7
    else:
        mant, ex = np.frexp(amax / 6.0)
        byte = np.where(mant > 0.5, ex, ex - 1) + 127
    byte = np.clip(np.where(amax > 0, byte, 1), 1, 254)
    scaled = (w * np.exp2(127.0 - byte)[:, None, :]).reshape(k, n).astype(np.float32)
    by_word = np.ascontiguousarray(scaled.reshape(k // 512, 128, 4, n).transpose(0, 1, 3, 2))
    if fmt == "e4m3":
        words = by_word.astype(ml_dtypes.float8_e4m3fn).view(np.uint8)
    else:
        c = by_word.astype(ml_dtypes.float4_e2m1fn).view(np.uint8) & 0xF
        words = (c[..., 0::2] | (c[..., 1::2] << 4)).reshape(k // 512, 128, 2 * n)
    return np.ascontiguousarray(words), np.ascontiguousarray(byte.astype(np.uint8).reshape(k // 512, 16, n))


def unpack_weight(words, scales, fmt):
    g, _, n = scales.shape
    words = np.ascontiguousarray(words).reshape(g, 128, n, -1)
    if fmt == "e4m3":
        vals = words.view(ml_dtypes.float8_e4m3fn).astype(np.float64)
    else:
        nib = np.empty((g, 128, n, 4), np.uint8)
        nib[..., 0::2] = words & 0xF
        nib[..., 1::2] = words >> 4
        vals = E2M1[nib]
    vals = vals * np.repeat(np.exp2(scales.astype(np.float64) - 127.0), 8, axis=1)[..., None]
    return vals.transpose(0, 1, 3, 2).reshape(g * 512, n)


def silu(v):
    return v / (1.0 + np.exp(-v))


B, N, T, D, NQ = 1, 512, 2048, 512, 256


def setup_inputs():
    n = np.random.standard_normal
    idx = np.random.permutation(T)[:B * N]
    s = mx_kscale(D)[:, None]
    kp = pack_weight(n((D, T)) / s, "e4m3")
    cp = pack_weight(n((D, T)) / s, "e4m3")
    return {
        "qT": (n((B, D, NQ)) * s * (1.00 / np.sqrt(D))).astype(np.float32),
        "k_words": kp[0],
        "k_scales": kp[1],
        "c_words": cp[0],
        "c_scales": cp[1],
        "offs": striped(idx),
    }


def reference(qT, k_words, k_scales, c_words, c_scales, offs):
    idx = unstriped(offs)
    pick = lambda x, which: x[:, which].reshape(x.shape[0], B, -1).transpose(1, 0, 2)
    k = unpack_weight(k_words, k_scales, "e4m3")
    kg = pick(k, idx)
    c = unpack_weight(c_words, c_scales, "e4m3")
    cg = pick(c, idx)
    qq = mxq(f64(qT), 1, "e4m3")
    a = qq.transpose(0, 2, 1) @ kg
    z = qq.transpose(0, 2, 1) @ cg
    y = silu(a) + z
    return y

@@ -1,0 +1,128 @@
+from contextlib import ExitStack
+
+import concourse.mybir as mybir
+
+F32 = mybir.dt.float32
+BF16 = mybir.dt.bfloat16
+I32 = mybir.dt.int32
+U32 = mybir.dt.uint32
+U16 = mybir.dt.uint16
+U8 = mybir.dt.uint8
+FP8X4 = mybir.dt.float8_e4m3fn_x4
+
+P = 128
+PACK = 4
+TOKENS = 2048
+SLOTS = 512
+QUERIES = 256
+HALF = SLOTS // 2
+Q_TILES = QUERIES // P
+LIST_COLS = SLOTS // 16
+C_ROW = 4
+
+FLOPS = 2 * 2 * QUERIES * SLOTS * P * PACK
+
+
+def tile_attend_swish_topk_kernel(tc, qT, k_words, k_scales, c_words, c_scales, offs, out):
+    nc = tc.nc
+    add = mybir.AluOpType.add
+    silu = mybir.ActivationFunctionType.Silu
+
+    with ExitStack() as ctx:
+        keep = ctx.enter_context(tc.tile_pool(name="keep", bufs=1))
+        psum = ctx.enter_context(tc.psum_pool(name="psum", bufs=1))
+
+        offsets = keep.tile([P, LIST_COLS], U16, name="offsets")
+        q_raw = keep.tile([P, PACK, QUERIES], F32, name="q_raw")
+        k_pool = keep.tile([P, TOKENS], I32, name="k_pool", align_bytes=64)
+        c_pool = keep.tile([P, TOKENS], I32, name="c_pool", align_bytes=64)
+        ks_pool = keep.tile([P, TOKENS], U8, name="ks_pool", align_bytes=64)
+        cs_pool = keep.tile([P, TOKENS], U8, name="cs_pool", align_bytes=64)
+
+        nc.vector.memset(ks_pool[:].bitcast(I32), 0)
+        nc.vector.memset(cs_pool[:].bitcast(I32), 0)
+
+        def load_scales(pool_tile, scales, first_row):
+            for r in range(4):
+                nc.sync.dma_start(
+                    out=pool_tile[first_row + r : P : 32, :].bitcast(I32),
+                    in_=scales[0, r:16:4, :].bitcast(I32),
+                )
+
+        def load_words(pool_tile, words):
+            nc.sync.dma_start(out=pool_tile[:], in_=words[0].rearrange("p n t -> p (n t)").bitcast(I32))
+
+        nc.sync.dma_start(offsets[:], offs)
+        nc.sync.dma_start(out=q_raw[:], in_=qT[0].rearrange("(p j) w -> p j w", j=PACK))
+        load_scales(ks_pool, k_scales, 0)
+        load_words(k_pool, k_words)
+        load_scales(cs_pool, c_scales, C_ROW)
+        load_words(c_pool, c_words)
+
+        ks_got = keep.tile([P, SLOTS], U8, name="ks_got", align_bytes=64)
+        nc.vector.tensor_copy(ks_got[:], ks_pool[:].indirect(offsets[:]))
+
+        q_grouped = keep.tile([P, QUERIES, PACK], BF16, name="q_grouped", align_bytes=64)
+        nc.scalar.copy(
+            out=q_grouped[:].rearrange("p (c i) t -> p c t i", i=4),
+            in_=q_raw[:].rearrange("p t (c i) -> p c t i", i=4),
+        )
+        q_codes = keep.tile([P, QUERIES], U32, name="q_codes", align_bytes=64)
+        q_scales = keep.tile([P, QUERIES], U8, name="q_scales", align_bytes=64)
+        nc.vector.quantize_mx(
+            out=q_codes[:].bitcast(FP8X4),
+            scales=q_scales[:],
+            in_=q_grouped[:].rearrange("p w j -> p (w j)"),
+        )
+
+        k_got = keep.tile([P, SLOTS], U32, name="k_got", align_bytes=64)
+        nc.vector.tensor_copy(k_got[:], k_pool[:].bitcast(U32).indirect(offsets[:]))
+
+        gated = keep.tile([P, Q_TILES, SLOTS], F32, name="gated")
+        for t in range(Q_TILES):
+            rows = slice(t * P, (t + 1) * P)
+            a_bank = psum.tile([P, SLOTS], F32, name="a_bank%d" % t)
+            nc.tensor.matmul_mx(
+                out=a_bank[:],
+                lhsT=q_codes[:, rows].bitcast(FP8X4),
+                lhsT_scale=q_scales[:, rows],
+                rhs=k_got[:].bitcast(FP8X4),
+                rhs_scale=ks_got[:],
+                start=True,
+                stop=True,
+            )
+            nc.scalar.activation(gated[:, t, :], a_bank[:], silu)
+
+        cs_got = keep.tile([P, SLOTS], U8, name="cs_got", align_bytes=64)
+        nc.vector.tensor_copy(cs_got[:], cs_pool[:].indirect(offsets[:]))
+
+        c_got = []
+        for h in range(2):
+            piece = keep.tile([P, HALF], U32, name="c_got%d" % h, align_bytes=64)
+            cols = slice(h * LIST_COLS // 2, (h + 1) * LIST_COLS // 2)
+            nc.vector.tensor_copy(piece[:], c_pool[:].bitcast(U32).indirect(offsets[:, cols]))
+            c_got.append(piece)
+
+        def z_pass(dest, t, h):
+            rows = slice(t * P, (t + 1) * P)
+            nc.tensor.matmul_mx(
+                out=dest,
+                lhsT=q_codes[:, rows].bitcast(FP8X4),
+                lhsT_scale=q_scales[:, rows],
+                rhs=c_got[h][:].bitcast(FP8X4),
+                rhs_scale=cs_got[C_ROW:P, h * HALF : (h + 1) * HALF],
+                start=True,
+                stop=True,
+            )
+
+        out_view = out[0].rearrange("(t p) n -> p t n", p=P)
+
+        for h in range(2):
+            slots = slice(h * HALF, (h + 1) * HALF)
+            for t in range(Q_TILES):
+                z_bank = psum.tile([P, HALF], F32, name="z_bank%d%d" % (h, t))
+                z_pass(z_bank[:], t, h)
+                result = keep.tile([P, HALF], F32, name="result%d%d" % (h, t))
+                nc.vector.tensor_tensor(result[:], z_bank[:], gated[:, t, slots], add)
+                queue = nc.scalar if t == 0 else nc.sync
+                queue.dma_start(out=out_view[:, t, slots], in_=result[:])

@@ -19,6 +19,8 @@ HALF = SLOTS // 2
 Q_TILES = QUERIES // P
 LIST_COLS = SLOTS // 16
 C_ROW = 4
+C_SPLIT = 3 * TOKENS // 8
+QUARTER = TOKENS // 4
 
 FLOPS = 2 * 2 * QUERIES * SLOTS * P * PACK
 
@@ -43,24 +45,41 @@ def tile_attend_swish_topk_kernel(tc, qT, k_words, k_scales, c_words, c_scales, 
         nc.vector.memset(cs_pool[:].bitcast(I32), 0)
 
         def load_scales(pool_tile, scales, first_row):
-            for r in range(4):
+            nc.sync.dma_start(out=pool_tile[first_row:P:8, :].bitcast(I32), in_=scales[0].bitcast(I32))
+
+        def load_words(pool_tile, words, tokens):
+            as_words = words[0].rearrange("p n t -> p (n t)").bitcast(I32)
+            nc.sync.dma_start(out=pool_tile[:, tokens], in_=as_words[:, tokens])
+
+        def gather_scales(pool_tile, name):
+            got = keep.tile([P, SLOTS], U8, name=name, align_bytes=64)
+            nc.vector.tensor_copy(got[:], pool_tile[:].indirect(offsets[:]))
+            return got
+
+        def move_rows(plane, got, first_row, rows):
+            for r in rows:
                 nc.sync.dma_start(
-                    out=pool_tile[first_row + r : P : 32, :].bitcast(I32),
-                    in_=scales[0, r:16:4, :].bitcast(I32),
+                    out=plane[first_row + r : P : 32, :].bitcast(I32),
+                    in_=got[first_row + 8 * r : P : 32, :].bitcast(I32),
                 )
 
-        def load_words(pool_tile, words):
-            nc.sync.dma_start(out=pool_tile[:], in_=words[0].rearrange("p n t -> p (n t)").bitcast(I32))
+        ks_got = keep.tile([P, SLOTS], U8, name="ks_plane", align_bytes=64)
+        cs_got = keep.tile([P, SLOTS], U8, name="cs_plane", align_bytes=64)
+        nc.vector.memset(ks_got[:].bitcast(I32), 0)
 
+        load_words(k_pool, k_words, slice(0, QUARTER))
         nc.sync.dma_start(offsets[:], offs)
-        nc.sync.dma_start(out=q_raw[:], in_=qT[0].rearrange("(p j) w -> p j w", j=PACK))
         load_scales(ks_pool, k_scales, 0)
-        load_words(k_pool, k_words)
+        nc.sync.dma_start(out=q_raw[:], in_=qT[0].rearrange("(p j) w -> p j w", j=PACK))
         load_scales(cs_pool, c_scales, C_ROW)
-        load_words(c_pool, c_words)
+        load_words(k_pool, k_words, slice(QUARTER, TOKENS))
+        load_words(c_pool, c_words, slice(0, C_SPLIT))
 
-        ks_got = keep.tile([P, SLOTS], U8, name="ks_got", align_bytes=64)
-        nc.vector.tensor_copy(ks_got[:], ks_pool[:].indirect(offsets[:]))
+        move_rows(ks_got, gather_scales(ks_pool, "ks_rows"), 0, range(4))
+        load_words(c_pool, c_words, slice(C_SPLIT, TOKENS))
+        cs_rows = gather_scales(cs_pool, "cs_rows")
+        nc.vector.tensor_copy(cs_got[:].bitcast(I32), cs_rows[:].bitcast(I32))
+        move_rows(cs_got, cs_rows, C_ROW, range(1, 4))
 
         q_grouped = keep.tile([P, QUERIES, PACK], BF16, name="q_grouped", align_bytes=64)
         nc.scalar.copy(
@@ -75,26 +94,28 @@ def tile_attend_swish_topk_kernel(tc, qT, k_words, k_scales, c_words, c_scales, 
             in_=q_grouped[:].rearrange("p w j -> p (w j)"),
         )
 
-        k_got = keep.tile([P, SLOTS], U32, name="k_got", align_bytes=64)
-        nc.vector.tensor_copy(k_got[:], k_pool[:].bitcast(U32).indirect(offsets[:]))
-
         gated = keep.tile([P, Q_TILES, SLOTS], F32, name="gated")
-        for t in range(Q_TILES):
-            rows = slice(t * P, (t + 1) * P)
-            a_bank = psum.tile([P, SLOTS], F32, name="a_bank%d" % t)
-            nc.tensor.matmul_mx(
-                out=a_bank[:],
-                lhsT=q_codes[:, rows].bitcast(FP8X4),
-                lhsT_scale=q_scales[:, rows],
-                rhs=k_got[:].bitcast(FP8X4),
-                rhs_scale=ks_got[:],
-                start=True,
-                stop=True,
-            )
-            nc.scalar.activation(gated[:, t, :], a_bank[:], silu)
-
-        cs_got = keep.tile([P, SLOTS], U8, name="cs_got", align_bytes=64)
-        nc.vector.tensor_copy(cs_got[:], cs_pool[:].indirect(offsets[:]))
+        k_got = []
+        for h in range(2):
+            piece = keep.tile([P, HALF], U32, name="k_got%d" % h, align_bytes=64)
+            cols = slice(h * LIST_COLS // 2, (h + 1) * LIST_COLS // 2)
+            nc.vector.tensor_copy(piece[:], k_pool[:].bitcast(U32).indirect(offsets[:, cols]))
+            k_got.append(piece)
+        for h in range(2):
+            slots = slice(h * HALF, (h + 1) * HALF)
+            for t in range(Q_TILES):
+                rows = slice(t * P, (t + 1) * P)
+                a_bank = psum.tile([P, HALF], F32, name="a_bank%d%d" % (h, t))
+                nc.tensor.matmul_mx(
+                    out=a_bank[:],
+                    lhsT=q_codes[:, rows].bitcast(FP8X4),
+                    lhsT_scale=q_scales[:, rows],
+                    rhs=k_got[h][:].bitcast(FP8X4),
+                    rhs_scale=ks_got[:, slots],
+                    start=True,
+                    stop=True,
+                )
+                nc.scalar.activation(gated[:, t, slots], a_bank[:], silu)
 
         c_got = []
         for h in range(2):

@@ -18,11 +18,14 @@ QUERIES = 256
 HALF = SLOTS // 2
 Q_TILES = QUERIES // P
 LIST_COLS = SLOTS // 16
-C_ROW = 4
-C_SPLIT = 3 * TOKENS // 8
-QUARTER = TOKENS // 4
+SCALE_ROWS = 16
+ROW_STEP = 4
+FIRST_SCALE_ROW = 32
+END_SCALE_ROW = FIRST_SCALE_ROW + ROW_STEP * SCALE_ROWS
 
 FLOPS = 2 * 2 * QUERIES * SLOTS * P * PACK
+K_LEAD = TOKENS // 4
+C_LEAD = 4 * TOKENS // 8
 
 
 def tile_attend_swish_topk_kernel(tc, qT, k_words, k_scales, c_words, c_scales, offs, out):
@@ -40,12 +43,16 @@ def tile_attend_swish_topk_kernel(tc, qT, k_words, k_scales, c_words, c_scales, 
         c_pool = keep.tile([P, TOKENS], I32, name="c_pool", align_bytes=64)
         ks_pool = keep.tile([P, TOKENS], U8, name="ks_pool", align_bytes=64)
         cs_pool = keep.tile([P, TOKENS], U8, name="cs_pool", align_bytes=64)
+        ks_plane = keep.tile([P, SLOTS], U8, name="ks_plane", align_bytes=64)
+        cs_plane = keep.tile([P, SLOTS], U8, name="cs_plane", align_bytes=64)
 
         nc.vector.memset(ks_pool[:].bitcast(I32), 0)
         nc.vector.memset(cs_pool[:].bitcast(I32), 0)
+        nc.vector.memset(ks_plane[:].bitcast(I32), 0)
+        nc.vector.memset(cs_plane[:].bitcast(I32), 0)
 
-        def load_scales(pool_tile, scales, first_row):
-            nc.sync.dma_start(out=pool_tile[first_row:P:8, :].bitcast(I32), in_=scales[0].bitcast(I32))
+        def load_scales(queue, pool_tile, scales):
+            queue.dma_start(out=pool_tile[FIRST_SCALE_ROW:END_SCALE_ROW:ROW_STEP, :].bitcast(I32), in_=scales[0].bitcast(I32))
 
         def load_words(pool_tile, words, tokens):
             as_words = words[0].rearrange("p n t -> p (n t)").bitcast(I32)
@@ -56,36 +63,30 @@ def tile_attend_swish_topk_kernel(tc, qT, k_words, k_scales, c_words, c_scales, 
             nc.vector.tensor_copy(got[:], pool_tile[:].indirect(offsets[:]))
             return got
 
-        def move_rows(plane, got, first_row, rows):
-            for r in rows:
+        def move_rows(plane, got):
+            for r in range(4):
                 nc.sync.dma_start(
-                    out=plane[first_row + r : P : 32, :].bitcast(I32),
-                    in_=got[first_row + 8 * r : P : 32, :].bitcast(I32),
+                    out=plane[r:P:32, :].bitcast(I32),
+                    in_=got[FIRST_SCALE_ROW + ROW_STEP * r : END_SCALE_ROW : 4 * ROW_STEP, :].bitcast(I32),
                 )
 
-        ks_got = keep.tile([P, SLOTS], U8, name="ks_plane", align_bytes=64)
-        cs_got = keep.tile([P, SLOTS], U8, name="cs_plane", align_bytes=64)
-        nc.vector.memset(ks_got[:].bitcast(I32), 0)
-
-        load_words(k_pool, k_words, slice(0, QUARTER))
+        load_words(k_pool, k_words, slice(0, K_LEAD))
         nc.sync.dma_start(offsets[:], offs)
-        load_scales(ks_pool, k_scales, 0)
+        load_scales(nc.sync, ks_pool, k_scales)
         nc.sync.dma_start(out=q_raw[:], in_=qT[0].rearrange("(p j) w -> p j w", j=PACK))
-        load_scales(cs_pool, c_scales, C_ROW)
-        load_words(k_pool, k_words, slice(QUARTER, TOKENS))
-        load_words(c_pool, c_words, slice(0, C_SPLIT))
+        load_scales(nc.sync, cs_pool, c_scales)
+        load_words(k_pool, k_words, slice(K_LEAD, TOKENS))
+        load_words(c_pool, c_words, slice(0, C_LEAD))
 
-        move_rows(ks_got, gather_scales(ks_pool, "ks_rows"), 0, range(4))
-        load_words(c_pool, c_words, slice(C_SPLIT, TOKENS))
-        cs_rows = gather_scales(cs_pool, "cs_rows")
-        nc.vector.tensor_copy(cs_got[:].bitcast(I32), cs_rows[:].bitcast(I32))
-        move_rows(cs_got, cs_rows, C_ROW, range(1, 4))
+        move_rows(ks_plane, gather_scales(ks_pool, "ks_rows"))
+        load_words(c_pool, c_words, slice(C_LEAD, TOKENS))
 
-        q_grouped = keep.tile([P, QUERIES, PACK], BF16, name="q_grouped", align_bytes=64)
+        q_grouped = keep.tile([P, QUERIES, PACK], BF16, name="q_grouped", tag="staging", align_bytes=64)
         nc.scalar.copy(
             out=q_grouped[:].rearrange("p (c i) t -> p c t i", i=4),
             in_=q_raw[:].rearrange("p t (c i) -> p c t i", i=4),
         )
+        move_rows(cs_plane, gather_scales(cs_pool, "cs_rows"))
         q_codes = keep.tile([P, QUERIES], U32, name="q_codes", align_bytes=64)
         q_scales = keep.tile([P, QUERIES], U8, name="q_scales", align_bytes=64)
         nc.vector.quantize_mx(
@@ -94,55 +95,42 @@ def tile_attend_swish_topk_kernel(tc, qT, k_words, k_scales, c_words, c_scales, 
             in_=q_grouped[:].rearrange("p w j -> p (w j)"),
         )
 
-        gated = keep.tile([P, Q_TILES, SLOTS], F32, name="gated")
-        k_got = []
-        for h in range(2):
-            piece = keep.tile([P, HALF], U32, name="k_got%d" % h, align_bytes=64)
-            cols = slice(h * LIST_COLS // 2, (h + 1) * LIST_COLS // 2)
-            nc.vector.tensor_copy(piece[:], k_pool[:].bitcast(U32).indirect(offsets[:, cols]))
-            k_got.append(piece)
-        for h in range(2):
-            slots = slice(h * HALF, (h + 1) * HALF)
-            for t in range(Q_TILES):
-                rows = slice(t * P, (t + 1) * P)
-                a_bank = psum.tile([P, HALF], F32, name="a_bank%d%d" % (h, t))
-                nc.tensor.matmul_mx(
-                    out=a_bank[:],
-                    lhsT=q_codes[:, rows].bitcast(FP8X4),
-                    lhsT_scale=q_scales[:, rows],
-                    rhs=k_got[h][:].bitcast(FP8X4),
-                    rhs_scale=ks_got[:, slots],
-                    start=True,
-                    stop=True,
+        def gather_words(pool_tile, tag):
+            got = keep.tile([P, SLOTS], U32, name="got", tag=tag, align_bytes=64)
+            for h in range(2):
+                cols = slice(h * LIST_COLS // 2, (h + 1) * LIST_COLS // 2)
+                nc.vector.tensor_copy(
+                    got[:, h * HALF : (h + 1) * HALF], pool_tile[:].bitcast(U32).indirect(offsets[:, cols])
                 )
-                nc.scalar.activation(gated[:, t, slots], a_bank[:], silu)
+            return got
 
-        c_got = []
-        for h in range(2):
-            piece = keep.tile([P, HALF], U32, name="c_got%d" % h, align_bytes=64)
-            cols = slice(h * LIST_COLS // 2, (h + 1) * LIST_COLS // 2)
-            nc.vector.tensor_copy(piece[:], c_pool[:].bitcast(U32).indirect(offsets[:, cols]))
-            c_got.append(piece)
-
-        def z_pass(dest, t, h):
+        def score(name, got, plane, h, t):
             rows = slice(t * P, (t + 1) * P)
+            bank = psum.tile([P, HALF], F32, name="%s%d%d" % (name, h, t))
             nc.tensor.matmul_mx(
-                out=dest,
+                out=bank[:],
                 lhsT=q_codes[:, rows].bitcast(FP8X4),
                 lhsT_scale=q_scales[:, rows],
-                rhs=c_got[h][:].bitcast(FP8X4),
-                rhs_scale=cs_got[C_ROW:P, h * HALF : (h + 1) * HALF],
+                rhs=got[:, h * HALF : (h + 1) * HALF].bitcast(FP8X4),
+                rhs_scale=plane[:, h * HALF : (h + 1) * HALF],
                 start=True,
                 stop=True,
             )
+            return bank
 
+        gated = keep.tile([P, Q_TILES, SLOTS], F32, name="gated")
+        k_got = gather_words(k_pool, "staging")
+        for h in range(2):
+            for t in range(Q_TILES):
+                a_bank = score("a_bank", k_got, ks_plane, h, t)
+                nc.scalar.activation(gated[:, t, h * HALF : (h + 1) * HALF], a_bank[:], silu)
+
+        c_got = gather_words(c_pool, "c_got")
         out_view = out[0].rearrange("(t p) n -> p t n", p=P)
-
         for h in range(2):
             slots = slice(h * HALF, (h + 1) * HALF)
             for t in range(Q_TILES):
-                z_bank = psum.tile([P, HALF], F32, name="z_bank%d%d" % (h, t))
-                z_pass(z_bank[:], t, h)
+                z_bank = score("z_bank", c_got, cs_plane, h, t)
                 result = keep.tile([P, HALF], F32, name="result%d%d" % (h, t))
                 nc.vector.tensor_tensor(result[:], z_bank[:], gated[:, t, slots], add)
                 queue = nc.scalar if t == 0 else nc.sync

@@ -133,5 +133,4 @@ def tile_attend_swish_topk_kernel(tc, qT, k_words, k_scales, c_words, c_scales, 
                 z_bank = score("z_bank", c_got, cs_plane, h, t)
                 result = keep.tile([P, HALF], F32, name="result%d%d" % (h, t))
                 nc.vector.tensor_tensor(result[:], z_bank[:], gated[:, t, slots], add)
-                queue = nc.scalar if t == 0 else nc.sync
-                queue.dma_start(out=out_view[:, t, slots], in_=result[:])
+                nc.sync.dma_start(out=out_view[:, t, slots], in_=result[:])

@@ -24,8 +24,7 @@ FIRST_SCALE_ROW = 32
 END_SCALE_ROW = FIRST_SCALE_ROW + ROW_STEP * SCALE_ROWS
 
 FLOPS = 2 * 2 * QUERIES * SLOTS * P * PACK
-K_LEAD = TOKENS // 4
-C_LEAD = 4 * TOKENS // 8
+C_LEAD = 5 * TOKENS // 8
 
 
 def tile_attend_swish_topk_kernel(tc, qT, k_words, k_scales, c_words, c_scales, offs, out):
@@ -70,12 +69,11 @@ def tile_attend_swish_topk_kernel(tc, qT, k_words, k_scales, c_words, c_scales, 
                     in_=got[FIRST_SCALE_ROW + ROW_STEP * r : END_SCALE_ROW : 4 * ROW_STEP, :].bitcast(I32),
                 )
 
-        load_words(k_pool, k_words, slice(0, K_LEAD))
+        nc.sync.dma_start(out=q_raw[:], in_=qT[0].rearrange("(p j) w -> p j w", j=PACK))
         nc.sync.dma_start(offsets[:], offs)
         load_scales(nc.sync, ks_pool, k_scales)
-        nc.sync.dma_start(out=q_raw[:], in_=qT[0].rearrange("(p j) w -> p j w", j=PACK))
         load_scales(nc.sync, cs_pool, c_scales)
-        load_words(k_pool, k_words, slice(K_LEAD, TOKENS))
+        load_words(k_pool, k_words, slice(0, TOKENS))
         load_words(c_pool, c_words, slice(0, C_LEAD))
 
         move_rows(ks_plane, gather_scales(ks_pool, "ks_rows"))
@@ -95,42 +93,42 @@ def tile_attend_swish_topk_kernel(tc, qT, k_words, k_scales, c_words, c_scales, 
             in_=q_grouped[:].rearrange("p w j -> p (w j)"),
         )
 
-        def gather_words(pool_tile, tag):
+        def gather_words(pool_tile, tag, pieces):
             got = keep.tile([P, SLOTS], U32, name="got", tag=tag, align_bytes=64)
-            for h in range(2):
-                cols = slice(h * LIST_COLS // 2, (h + 1) * LIST_COLS // 2)
+            width = SLOTS // pieces
+            for h in range(pieces):
+                cols = slice(h * width // 16, (h + 1) * width // 16)
                 nc.vector.tensor_copy(
-                    got[:, h * HALF : (h + 1) * HALF], pool_tile[:].bitcast(U32).indirect(offsets[:, cols])
+                    got[:, h * width : (h + 1) * width], pool_tile[:].bitcast(U32).indirect(offsets[:, cols])
                 )
             return got
 
-        def score(name, got, plane, h, t):
+        def score(name, got, plane, t, slots):
             rows = slice(t * P, (t + 1) * P)
-            bank = psum.tile([P, HALF], F32, name="%s%d%d" % (name, h, t))
+            bank = psum.tile([P, slots.stop - slots.start], F32, name=name)
             nc.tensor.matmul_mx(
                 out=bank[:],
                 lhsT=q_codes[:, rows].bitcast(FP8X4),
                 lhsT_scale=q_scales[:, rows],
-                rhs=got[:, h * HALF : (h + 1) * HALF].bitcast(FP8X4),
-                rhs_scale=plane[:, h * HALF : (h + 1) * HALF],
+                rhs=got[:, slots].bitcast(FP8X4),
+                rhs_scale=plane[:, slots],
                 start=True,
                 stop=True,
             )
             return bank
 
         gated = keep.tile([P, Q_TILES, SLOTS], F32, name="gated")
-        k_got = gather_words(k_pool, "staging")
-        for h in range(2):
-            for t in range(Q_TILES):
-                a_bank = score("a_bank", k_got, ks_plane, h, t)
-                nc.scalar.activation(gated[:, t, h * HALF : (h + 1) * HALF], a_bank[:], silu)
+        k_got = gather_words(k_pool, "staging", 1)
+        for t in range(Q_TILES):
+            a_bank = score("a_bank%d" % t, k_got, ks_plane, t, slice(0, SLOTS))
+            nc.scalar.activation(gated[:, t, :], a_bank[:], silu)
 
-        c_got = gather_words(c_pool, "c_got")
+        c_got = gather_words(c_pool, "c_got", 2)
         out_view = out[0].rearrange("(t p) n -> p t n", p=P)
         for h in range(2):
             slots = slice(h * HALF, (h + 1) * HALF)
             for t in range(Q_TILES):
-                z_bank = score("z_bank", c_got, cs_plane, h, t)
+                z_bank = score("z_bank%d%d" % (h, t), c_got, cs_plane, t, slots)
                 result = keep.tile([P, HALF], F32, name="result%d%d" % (h, t))
                 nc.vector.tensor_tensor(result[:], z_bank[:], gated[:, t, slots], add)
                 nc.sync.dma_start(out=out_view[:, t, slots], in_=result[:])

@@ -125,10 +125,10 @@ def tile_attend_swish_topk_kernel(tc, qT, k_words, k_scales, c_words, c_scales, 
 
         c_got = gather_words(c_pool, "c_got", 2)
         out_view = out[0].rearrange("(t p) n -> p t n", p=P)
-        for h in range(2):
-            slots = slice(h * HALF, (h + 1) * HALF)
-            for t in range(Q_TILES):
-                z_bank = score("z_bank%d%d" % (h, t), c_got, cs_plane, t, slots)
-                result = keep.tile([P, HALF], F32, name="result%d%d" % (h, t))
-                nc.vector.tensor_tensor(result[:], z_bank[:], gated[:, t, slots], add)
-                nc.sync.dma_start(out=out_view[:, t, slots], in_=result[:])
+        result = keep.tile([P, Q_TILES, SLOTS], F32, name="result")
+        for t, lo, hi, store_from in [(0, 0, P, 0), (0, P, HALF, P), (1, 0, HALF, 0), (0, HALF, SLOTS, HALF), (1, HALF, SLOTS, HALF)]:
+            slots = slice(lo, hi)
+            z_bank = score("z_bank%d_%d" % (t, lo), c_got, cs_plane, t, slots)
+            nc.vector.tensor_tensor(result[:, t, slots], z_bank[:], gated[:, t, slots], add)
+            if store_from is not None:
+                nc.sync.dma_start(out=out_view[:, t, store_from:hi], in_=result[:, t, store_from:hi])

@@ -62,12 +62,14 @@ def tile_attend_swish_topk_kernel(tc, qT, k_words, k_scales, c_words, c_scales, 
             nc.vector.tensor_copy(got[:], pool_tile[:].indirect(offsets[:]))
             return got
 
-        def move_rows(plane, got):
-            for r in range(4):
+        def move_rows(plane, got, pieces):
+            for r, slots in pieces:
                 nc.sync.dma_start(
-                    out=plane[r:P:32, :].bitcast(I32),
-                    in_=got[FIRST_SCALE_ROW + ROW_STEP * r : END_SCALE_ROW : 4 * ROW_STEP, :].bitcast(I32),
+                    out=plane[r:P:32, slots].bitcast(I32),
+                    in_=got[FIRST_SCALE_ROW + ROW_STEP * r : END_SCALE_ROW : 4 * ROW_STEP, slots].bitcast(I32),
                 )
+
+        whole, first, second = slice(0, SLOTS), slice(0, HALF), slice(HALF, SLOTS)
 
         nc.sync.dma_start(out=q_raw[:], in_=qT[0].rearrange("(p j) w -> p j w", j=PACK))
         nc.sync.dma_start(offsets[:], offs)
@@ -76,7 +78,7 @@ def tile_attend_swish_topk_kernel(tc, qT, k_words, k_scales, c_words, c_scales, 
         load_words(k_pool, k_words, slice(0, TOKENS))
         load_words(c_pool, c_words, slice(0, C_LEAD))
 
-        move_rows(ks_plane, gather_scales(ks_pool, "ks_rows"))
+        move_rows(ks_plane, gather_scales(ks_pool, "ks_rows"), [(r, whole) for r in range(4)])
         load_words(c_pool, c_words, slice(C_LEAD, TOKENS))
 
         q_grouped = keep.tile([P, QUERIES, PACK], BF16, name="q_grouped", tag="staging", align_bytes=64)
@@ -84,7 +86,11 @@ def tile_attend_swish_topk_kernel(tc, qT, k_words, k_scales, c_words, c_scales, 
             out=q_grouped[:].rearrange("p (c i) t -> p c t i", i=4),
             in_=q_raw[:].rearrange("p t (c i) -> p c t i", i=4),
         )
-        move_rows(cs_plane, gather_scales(cs_pool, "cs_rows"))
+        move_rows(
+            cs_plane,
+            gather_scales(cs_pool, "cs_rows"),
+            [(0, whole)] + [(r, slots) for slots in (first, second) for r in range(1, 4)],
+        )
         q_codes = keep.tile([P, QUERIES], U32, name="q_codes", align_bytes=64)
         q_scales = keep.tile([P, QUERIES], U8, name="q_scales", align_bytes=64)
         nc.vector.quantize_mx(
@@ -126,7 +132,7 @@ def tile_attend_swish_topk_kernel(tc, qT, k_words, k_scales, c_words, c_scales, 
         c_got = gather_words(c_pool, "c_got", 2)
         out_view = out[0].rearrange("(t p) n -> p t n", p=P)
         result = keep.tile([P, Q_TILES, SLOTS], F32, name="result")
-        for t, lo, hi, store_from in [(0, 0, P, 0), (0, P, HALF, P), (1, 0, HALF, 0), (0, HALF, SLOTS, HALF), (1, HALF, SLOTS, HALF)]:
+        for t, lo, hi, store_from in [(0, 0, P, 0), (0, P, HALF, P), (1, 0, P, None), (1, P, HALF, 0), (0, HALF, SLOTS, HALF), (1, HALF, SLOTS, HALF)]:
             slots = slice(lo, hi)
             z_bank = score("z_bank%d_%d" % (t, lo), c_got, cs_plane, t, slots)
             nc.vector.tensor_tensor(result[:, t, slots], z_bank[:], gated[:, t, slots], add)

@@ -24,7 +24,7 @@ FIRST_SCALE_ROW = 32
 END_SCALE_ROW = FIRST_SCALE_ROW + ROW_STEP * SCALE_ROWS
 
 FLOPS = 2 * 2 * QUERIES * SLOTS * P * PACK
-C_LEAD = 5 * TOKENS // 8
+C_LEAD = 9 * TOKENS // 16
 
 
 def tile_attend_swish_topk_kernel(tc, qT, k_words, k_scales, c_words, c_scales, offs, out):
@@ -111,7 +111,7 @@ def tile_attend_swish_topk_kernel(tc, qT, k_words, k_scales, c_words, c_scales, 
 
         def score(name, got, plane, t, slots):
             rows = slice(t * P, (t + 1) * P)
-            bank = psum.tile([P, slots.stop - slots.start], F32, name=name)
+            bank = psum.tile([P, slots.stop - slots.start], F32, name="bank", tag=name)
             nc.tensor.matmul_mx(
                 out=bank[:],
                 lhsT=q_codes[:, rows].bitcast(FP8X4),
@@ -124,17 +124,26 @@ def tile_attend_swish_topk_kernel(tc, qT, k_words, k_scales, c_words, c_scales, 
             return bank
 
         gated = keep.tile([P, Q_TILES, SLOTS], F32, name="gated")
-        k_got = gather_words(k_pool, "staging", 1)
-        for t in range(Q_TILES):
-            a_bank = score("a_bank%d" % t, k_got, ks_plane, t, slice(0, SLOTS))
-            nc.scalar.activation(gated[:, t, :], a_bank[:], silu)
+        k_got = gather_words(k_pool, "staging", 2)
+        for bank, t, lo, hi in [(0, 0, 0, P), (1, 1, 0, HALF), (2, 0, P, HALF), (3, 0, HALF, SLOTS), (0, 1, HALF, SLOTS)]:
+            a_bank = score("bank%d" % bank, k_got, ks_plane, t, slice(lo, hi))
+            nc.scalar.activation(gated[:, t, lo:hi], a_bank[:], silu)
 
         c_got = gather_words(c_pool, "c_got", 2)
         out_view = out[0].rearrange("(t p) n -> p t n", p=P)
         result = keep.tile([P, Q_TILES, SLOTS], F32, name="result")
-        for t, lo, hi, store_from in [(0, 0, P, 0), (0, P, HALF, P), (1, 0, P, None), (1, P, HALF, 0), (0, HALF, SLOTS, HALF), (1, HALF, SLOTS, HALF)]:
+        for bank, t, lo, hi, store_from in [
+            (4, 0, 0, P, 0),
+            (2, 0, P, HALF, P),
+            (1, 1, 0, P, None),
+            (3, 1, P, HALF, 0),
+            (5, 0, HALF, HALF + P, None),
+            (7, 0, HALF + P, SLOTS, HALF),
+            (0, 1, HALF, HALF + P, None),
+            (6, 1, HALF + P, SLOTS, HALF),
+        ]:
             slots = slice(lo, hi)
-            z_bank = score("z_bank%d_%d" % (t, lo), c_got, cs_plane, t, slots)
+            z_bank = score("bank%d" % bank, c_got, cs_plane, t, slots)
             nc.vector.tensor_tensor(result[:, t, slots], z_bank[:], gated[:, t, slots], add)
             if store_from is not None:
                 nc.sync.dma_start(out=out_view[:, t, store_from:hi], in_=result[:, t, store_from:hi])

@@ -49,6 +49,8 @@ def tile_attend_swish_topk_kernel(tc, qT, k_words, k_scales, c_words, c_scales, 
         nc.vector.memset(cs_pool[:].bitcast(I32), 0)
         nc.vector.memset(ks_plane[:].bitcast(I32), 0)
         nc.vector.memset(cs_plane[:].bitcast(I32), 0)
+        q_codes = keep.tile([P, SLOTS], U32, name="q_codes", align_bytes=64)
+        nc.vector.memset(q_codes[:, QUERIES:].bitcast(I32), 0)
 
         def load_scales(queue, pool_tile, scales):
             queue.dma_start(out=pool_tile[FIRST_SCALE_ROW:END_SCALE_ROW:ROW_STEP, :].bitcast(I32), in_=scales[0].bitcast(I32))
@@ -78,7 +80,8 @@ def tile_attend_swish_topk_kernel(tc, qT, k_words, k_scales, c_words, c_scales, 
         load_words(k_pool, k_words, slice(0, TOKENS))
         load_words(c_pool, c_words, slice(0, C_LEAD))
 
-        move_rows(ks_plane, gather_scales(ks_pool, "ks_rows"), [(r, whole) for r in range(4)])
+        ks_rows = gather_scales(ks_pool, "ks_rows")
+        move_rows(ks_plane, ks_rows, [(r, whole) for r in range(4)])
         load_words(c_pool, c_words, slice(C_LEAD, TOKENS))
 
         q_grouped = keep.tile([P, QUERIES, PACK], BF16, name="q_grouped", tag="staging", align_bytes=64)
@@ -91,10 +94,9 @@ def tile_attend_swish_topk_kernel(tc, qT, k_words, k_scales, c_words, c_scales, 
             gather_scales(cs_pool, "cs_rows"),
             [(0, whole)] + [(r, slots) for slots in (first, second) for r in range(1, 4)],
         )
-        q_codes = keep.tile([P, QUERIES], U32, name="q_codes", align_bytes=64)
         q_scales = keep.tile([P, QUERIES], U8, name="q_scales", align_bytes=64)
         nc.vector.quantize_mx(
-            out=q_codes[:].bitcast(FP8X4),
+            out=q_codes[:, :QUERIES].bitcast(FP8X4),
             scales=q_scales[:],
             in_=q_grouped[:].rearrange("p w j -> p (w j)"),
         )
@@ -124,6 +126,7 @@ def tile_attend_swish_topk_kernel(tc, qT, k_words, k_scales, c_words, c_scales, 
             return bank
 
         gated = keep.tile([P, Q_TILES, SLOTS], F32, name="gated")
+        score("bank7", q_codes, ks_rows, 0, whole)
         k_got = gather_words(k_pool, "staging", 2)
         for bank, t, lo, hi in [(0, 0, 0, P), (1, 1, 0, HALF), (2, 0, P, HALF), (3, 0, HALF, SLOTS), (0, 1, HALF, SLOTS)]:
             a_bank = score("bank%d" % bank, k_got, ks_plane, t, slice(lo, hi))

@@ -17,26 +17,29 @@ SLOTS = 512
 QUERIES = 256
 HALF = SLOTS // 2
 Q_TILES = QUERIES // P
-LIST_COLS = SLOTS // 16
+LIST_GROUP = 16
+QUADRANT = 32
+PLANE_ROWS = 4
 SCALE_ROWS = 16
 ROW_STEP = 4
 FIRST_SCALE_ROW = 32
 END_SCALE_ROW = FIRST_SCALE_ROW + ROW_STEP * SCALE_ROWS
+C_LEAD = 9 * TOKENS // 16
 
 FLOPS = 2 * 2 * QUERIES * SLOTS * P * PACK
-C_LEAD = 9 * TOKENS // 16
 
 
 def tile_attend_swish_topk_kernel(tc, qT, k_words, k_scales, c_words, c_scales, offs, out):
     nc = tc.nc
     add = mybir.AluOpType.add
     silu = mybir.ActivationFunctionType.Silu
+    whole, first, second = slice(0, SLOTS), slice(0, HALF), slice(HALF, SLOTS)
 
     with ExitStack() as ctx:
         keep = ctx.enter_context(tc.tile_pool(name="keep", bufs=1))
         psum = ctx.enter_context(tc.psum_pool(name="psum", bufs=1))
 
-        offsets = keep.tile([P, LIST_COLS], U16, name="offsets")
+        offsets = keep.tile([P, SLOTS // LIST_GROUP], U16, name="offsets")
         q_raw = keep.tile([P, PACK, QUERIES], F32, name="q_raw")
         k_pool = keep.tile([P, TOKENS], I32, name="k_pool", align_bytes=64)
         c_pool = keep.tile([P, TOKENS], I32, name="c_pool", align_bytes=64)
@@ -52,36 +55,33 @@ def tile_attend_swish_topk_kernel(tc, qT, k_words, k_scales, c_words, c_scales, 
         q_codes = keep.tile([P, SLOTS], U32, name="q_codes", align_bytes=64)
         nc.vector.memset(q_codes[:, QUERIES:].bitcast(I32), 0)
 
-        def load_scales(queue, pool_tile, scales):
-            queue.dma_start(out=pool_tile[FIRST_SCALE_ROW:END_SCALE_ROW:ROW_STEP, :].bitcast(I32), in_=scales[0].bitcast(I32))
+        def load_scales(pool_tile, scales):
+            rows = pool_tile[FIRST_SCALE_ROW:END_SCALE_ROW:ROW_STEP, :]
+            nc.sync.dma_start(out=rows.bitcast(I32), in_=scales[0].bitcast(I32))
 
         def load_words(pool_tile, words, tokens):
             as_words = words[0].rearrange("p n t -> p (n t)").bitcast(I32)
             nc.sync.dma_start(out=pool_tile[:, tokens], in_=as_words[:, tokens])
 
         def gather_scales(pool_tile, name):
-            got = keep.tile([P, SLOTS], U8, name=name, align_bytes=64)
-            nc.vector.tensor_copy(got[:], pool_tile[:].indirect(offsets[:]))
-            return got
+            rows = keep.tile([P, SLOTS], U8, name=name, align_bytes=64)
+            nc.vector.tensor_copy(rows[:], pool_tile[:].indirect(offsets[:]))
+            return rows
 
-        def move_rows(plane, got, pieces):
-            for r, slots in pieces:
-                nc.sync.dma_start(
-                    out=plane[r:P:32, slots].bitcast(I32),
-                    in_=got[FIRST_SCALE_ROW + ROW_STEP * r : END_SCALE_ROW : 4 * ROW_STEP, slots].bitcast(I32),
-                )
-
-        whole, first, second = slice(0, SLOTS), slice(0, HALF), slice(HALF, SLOTS)
+        def move_rows(plane, rows, moves):
+            for queue, r, slots in moves:
+                source = rows[FIRST_SCALE_ROW + ROW_STEP * r : END_SCALE_ROW : PLANE_ROWS * ROW_STEP, slots]
+                queue.dma_start(out=plane[r:P:QUADRANT, slots].bitcast(I32), in_=source.bitcast(I32))
 
         nc.sync.dma_start(out=q_raw[:], in_=qT[0].rearrange("(p j) w -> p j w", j=PACK))
         nc.sync.dma_start(offsets[:], offs)
-        load_scales(nc.sync, ks_pool, k_scales)
-        load_scales(nc.sync, cs_pool, c_scales)
+        load_scales(ks_pool, k_scales)
+        load_scales(cs_pool, c_scales)
         load_words(k_pool, k_words, slice(0, TOKENS))
         load_words(c_pool, c_words, slice(0, C_LEAD))
 
         ks_rows = gather_scales(ks_pool, "ks_rows")
-        move_rows(ks_plane, ks_rows, [(r, whole) for r in range(4)])
+        move_rows(ks_plane, ks_rows, [(nc.sync, r, whole) for r in range(1, PLANE_ROWS)])
         load_words(c_pool, c_words, slice(C_LEAD, TOKENS))
 
         q_grouped = keep.tile([P, QUERIES, PACK], BF16, name="q_grouped", tag="staging", align_bytes=64)
@@ -89,11 +89,11 @@ def tile_attend_swish_topk_kernel(tc, qT, k_words, k_scales, c_words, c_scales, 
             out=q_grouped[:].rearrange("p (c i) t -> p c t i", i=4),
             in_=q_raw[:].rearrange("p t (c i) -> p c t i", i=4),
         )
-        move_rows(
-            cs_plane,
-            gather_scales(cs_pool, "cs_rows"),
-            [(0, whole)] + [(r, slots) for slots in (first, second) for r in range(1, 4)],
-        )
+        move_rows(ks_plane, ks_rows, [(nc.scalar, 0, whole)])
+        cs_rows = gather_scales(cs_pool, "cs_rows")
+        halved = [(nc.sync, r, slots) for slots in (first, second) for r in range(1, PLANE_ROWS)]
+        move_rows(cs_plane, cs_rows, [(nc.sync, 0, whole)] + halved)
+
         q_scales = keep.tile([P, QUERIES], U8, name="q_scales", align_bytes=64)
         nc.vector.quantize_mx(
             out=q_codes[:, :QUERIES].bitcast(FP8X4),
@@ -101,52 +101,48 @@ def tile_attend_swish_topk_kernel(tc, qT, k_words, k_scales, c_words, c_scales, 
             in_=q_grouped[:].rearrange("p w j -> p (w j)"),
         )
 
-        def gather_words(pool_tile, tag, pieces):
-            got = keep.tile([P, SLOTS], U32, name="got", tag=tag, align_bytes=64)
-            width = SLOTS // pieces
-            for h in range(pieces):
-                cols = slice(h * width // 16, (h + 1) * width // 16)
-                nc.vector.tensor_copy(
-                    got[:, h * width : (h + 1) * width], pool_tile[:].bitcast(U32).indirect(offsets[:, cols])
-                )
-            return got
+        def gather_words(pool_tile, tag):
+            gathered = keep.tile([P, SLOTS], U32, name="got", tag=tag, align_bytes=64)
+            for slots in (first, second):
+                entries = offsets[:, slots.start // LIST_GROUP : slots.stop // LIST_GROUP]
+                nc.vector.tensor_copy(gathered[:, slots], pool_tile[:].bitcast(U32).indirect(entries))
+            return gathered
 
-        def score(name, got, plane, t, slots):
-            rows = slice(t * P, (t + 1) * P)
-            bank = psum.tile([P, slots.stop - slots.start], F32, name="bank", tag=name)
+        def score(bank, words, plane, t, slots):
+            queries = slice(t * P, (t + 1) * P)
+            scores = psum.tile([P, slots.stop - slots.start], F32, name="bank", tag="bank%d" % bank)
             nc.tensor.matmul_mx(
-                out=bank[:],
-                lhsT=q_codes[:, rows].bitcast(FP8X4),
-                lhsT_scale=q_scales[:, rows],
-                rhs=got[:, slots].bitcast(FP8X4),
+                out=scores[:],
+                lhsT=q_codes[:, queries].bitcast(FP8X4),
+                lhsT_scale=q_scales[:, queries],
+                rhs=words[:, slots].bitcast(FP8X4),
                 rhs_scale=plane[:, slots],
                 start=True,
                 stop=True,
             )
-            return bank
+            return scores
 
         gated = keep.tile([P, Q_TILES, SLOTS], F32, name="gated")
-        score("bank7", q_codes, ks_rows, 0, whole)
-        k_got = gather_words(k_pool, "staging", 2)
-        for bank, t, lo, hi in [(0, 0, 0, P), (1, 1, 0, HALF), (2, 0, P, HALF), (3, 0, HALF, SLOTS), (0, 1, HALF, SLOTS)]:
-            a_bank = score("bank%d" % bank, k_got, ks_plane, t, slice(lo, hi))
-            nc.scalar.activation(gated[:, t, lo:hi], a_bank[:], silu)
+        score(7, q_codes, ks_rows, 0, whole)
 
-        c_got = gather_words(c_pool, "c_got", 2)
+        k_got = gather_words(k_pool, "staging")
+
+        a_passes = [(0, 0, 0, P), (1, 1, 0, HALF), (2, 0, P, HALF), (3, 0, HALF, SLOTS), (0, 1, HALF, SLOTS)]
+        for bank, t, lo, hi in a_passes:
+            a_scores = score(bank, k_got, ks_plane, t, slice(lo, hi))
+            nc.scalar.activation(gated[:, t, lo:hi], a_scores[:], silu)
+
+        c_got = gather_words(c_pool, "c_got")
         out_view = out[0].rearrange("(t p) n -> p t n", p=P)
         result = keep.tile([P, Q_TILES, SLOTS], F32, name="result")
-        for bank, t, lo, hi, store_from in [
-            (4, 0, 0, P, 0),
-            (2, 0, P, HALF, P),
-            (1, 1, 0, P, None),
-            (3, 1, P, HALF, 0),
-            (5, 0, HALF, HALF + P, None),
-            (7, 0, HALF + P, SLOTS, HALF),
-            (0, 1, HALF, HALF + P, None),
-            (6, 1, HALF + P, SLOTS, HALF),
-        ]:
-            slots = slice(lo, hi)
-            z_bank = score("bank%d" % bank, c_got, cs_plane, t, slots)
-            nc.vector.tensor_tensor(result[:, t, slots], z_bank[:], gated[:, t, slots], add)
-            if store_from is not None:
-                nc.sync.dma_start(out=out_view[:, t, store_from:hi], in_=result[:, t, store_from:hi])
+        z_passes = [(t, lo) for half in (first, second) for t in range(Q_TILES) for lo in (half.start, half.start + P)]
+        z_banks = [4, 2, 1, 3, 5, 7, 0, 6]
+        for bank, (t, lo) in zip(z_banks, z_passes):
+            slots = slice(lo, lo + P)
+            z_scores = score(bank, c_got, cs_plane, t, slots)
+            nc.vector.tensor_tensor(result[:, t, slots], z_scores[:], gated[:, t, slots], add)
+            if t == 0 and lo < HALF:
+                nc.sync.dma_start(out=out_view[:, t, slots], in_=result[:, t, slots])
+            elif slots.stop % HALF == 0:
+                done = slice(slots.stop - HALF, slots.stop)
+                nc.sync.dma_start(out=out_view[:, t, done], in_=result[:, t, done])

@@ -52,8 +52,7 @@ def tile_attend_swish_topk_kernel(tc, qT, k_words, k_scales, c_words, c_scales, 
         nc.vector.memset(cs_pool[:].bitcast(I32), 0)
         nc.vector.memset(ks_plane[:].bitcast(I32), 0)
         nc.vector.memset(cs_plane[:].bitcast(I32), 0)
-        q_codes = keep.tile([P, SLOTS], U32, name="q_codes", align_bytes=64)
-        nc.vector.memset(q_codes[:, QUERIES:].bitcast(I32), 0)
+        q_codes = keep.tile([P, QUERIES], U32, name="q_codes", align_bytes=64)
 
         def load_scales(pool_tile, scales):
             rows = pool_tile[FIRST_SCALE_ROW:END_SCALE_ROW:ROW_STEP, :]
@@ -96,7 +95,7 @@ def tile_attend_swish_topk_kernel(tc, qT, k_words, k_scales, c_words, c_scales, 
 
         q_scales = keep.tile([P, QUERIES], U8, name="q_scales", align_bytes=64)
         nc.vector.quantize_mx(
-            out=q_codes[:, :QUERIES].bitcast(FP8X4),
+            out=q_codes[:].bitcast(FP8X4),
             scales=q_scales[:],
             in_=q_grouped[:].rearrange("p w j -> p (w j)"),
         )
@@ -123,8 +122,6 @@ def tile_attend_swish_topk_kernel(tc, qT, k_words, k_scales, c_words, c_scales, 
             return scores
 
         gated = keep.tile([P, Q_TILES, SLOTS], F32, name="gated")
-        score(7, q_codes, ks_rows, 0, whole)
-
         k_got = gather_words(k_pool, "staging")
 
         a_passes = [(0, 0, 0, P), (1, 1, 0, HALF), (2, 0, P, HALF), (3, 0, HALF, SLOTS), (0, 1, HALF, SLOTS)]

from contextlib import ExitStack

import concourse.mybir as mybir

F32 = mybir.dt.float32
BF16 = mybir.dt.bfloat16
I32 = mybir.dt.int32
U32 = mybir.dt.uint32
U16 = mybir.dt.uint16
U8 = mybir.dt.uint8
FP8X4 = mybir.dt.float8_e4m3fn_x4

P = 128
PACK = 4
TOKENS = 2048
SLOTS = 512
QUERIES = 256
HALF = SLOTS // 2
Q_TILES = QUERIES // P
LIST_GROUP = 16
QUADRANT = 32
PLANE_ROWS = 4
SCALE_ROWS = 16
ROW_STEP = 4
FIRST_SCALE_ROW = 32
END_SCALE_ROW = FIRST_SCALE_ROW + ROW_STEP * SCALE_ROWS
C_LEAD = 9 * TOKENS // 16

FLOPS = 2 * 2 * QUERIES * SLOTS * P * PACK


def tile_attend_swish_topk_kernel(tc, qT, k_words, k_scales, c_words, c_scales, offs, out):
    nc = tc.nc
    add = mybir.AluOpType.add
    silu = mybir.ActivationFunctionType.Silu
    whole, first, second = slice(0, SLOTS), slice(0, HALF), slice(HALF, SLOTS)

    with ExitStack() as ctx:
        keep = ctx.enter_context(tc.tile_pool(name="keep", bufs=1))
        psum = ctx.enter_context(tc.psum_pool(name="psum", bufs=1))

        offsets = keep.tile([P, SLOTS // LIST_GROUP], U16, name="offsets")
        q_raw = keep.tile([P, PACK, QUERIES], F32, name="q_raw")
        k_pool = keep.tile([P, TOKENS], I32, name="k_pool", align_bytes=64)
        c_pool = keep.tile([P, TOKENS], I32, name="c_pool", align_bytes=64)
        ks_pool = keep.tile([P, TOKENS], U8, name="ks_pool", align_bytes=64)
        cs_pool = keep.tile([P, TOKENS], U8, name="cs_pool", align_bytes=64)
        ks_plane = keep.tile([P, SLOTS], U8, name="ks_plane", align_bytes=64)
        cs_plane = keep.tile([P, SLOTS], U8, name="cs_plane", align_bytes=64)

        nc.vector.memset(ks_pool[:].bitcast(I32), 0)
        nc.vector.memset(cs_pool[:].bitcast(I32), 0)
        nc.vector.memset(ks_plane[:].bitcast(I32), 0)
        nc.vector.memset(cs_plane[:].bitcast(I32), 0)
        q_codes = keep.tile([P, QUERIES], U32, name="q_codes", align_bytes=64)

        def load_scales(pool_tile, scales):
            rows = pool_tile[FIRST_SCALE_ROW:END_SCALE_ROW:ROW_STEP, :]
            nc.sync.dma_start(out=rows.bitcast(I32), in_=scales[0].bitcast(I32))

        def load_words(pool_tile, words, tokens):
            as_words = words[0].rearrange("p n t -> p (n t)").bitcast(I32)
            nc.sync.dma_start(out=pool_tile[:, tokens], in_=as_words[:, tokens])

        def gather_scales(pool_tile, name):
            rows = keep.tile([P, SLOTS], U8, name=name, align_bytes=64)
            nc.vector.tensor_copy(rows[:], pool_tile[:].indirect(offsets[:]))
            return rows

        def move_rows(plane, rows, moves):
            for queue, r, slots in moves:
                source = rows[FIRST_SCALE_ROW + ROW_STEP * r : END_SCALE_ROW : PLANE_ROWS * ROW_STEP, slots]
                queue.dma_start(out=plane[r:P:QUADRANT, slots].bitcast(I32), in_=source.bitcast(I32))

        nc.sync.dma_start(out=q_raw[:], in_=qT[0].rearrange("(p j) w -> p j w", j=PACK))
        nc.sync.dma_start(offsets[:], offs)
        load_scales(ks_pool, k_scales)
        load_scales(cs_pool, c_scales)
        load_words(k_pool, k_words, slice(0, TOKENS))
        load_words(c_pool, c_words, slice(0, C_LEAD))

        ks_rows = gather_scales(ks_pool, "ks_rows")
        move_rows(ks_plane, ks_rows, [(nc.sync, r, whole) for r in range(1, PLANE_ROWS)])
        load_words(c_pool, c_words, slice(C_LEAD, TOKENS))

        q_grouped = keep.tile([P, QUERIES, PACK], BF16, name="q_grouped", tag="staging", align_bytes=64)
        nc.scalar.copy(
            out=q_grouped[:].rearrange("p (c i) t -> p c t i", i=4),
            in_=q_raw[:].rearrange("p t (c i) -> p c t i", i=4),
        )
        move_rows(ks_plane, ks_rows, [(nc.scalar, 0, whole)])
        cs_rows = gather_scales(cs_pool, "cs_rows")
        halved = [(nc.sync, r, slots) for slots in (first, second) for r in range(1, PLANE_ROWS)]
        move_rows(cs_plane, cs_rows, [(nc.sync, 0, whole)] + halved)

        q_scales = keep.tile([P, QUERIES], U8, name="q_scales", align_bytes=64)
        nc.vector.quantize_mx(
            out=q_codes[:].bitcast(FP8X4),
            scales=q_scales[:],
            in_=q_grouped[:].rearrange("p w j -> p (w j)"),
        )

        def gather_words(pool_tile, tag):
            gathered = keep.tile([P, SLOTS], U32, name="got", tag=tag, align_bytes=64)
            for slots in (first, second):
                entries = offsets[:, slots.start // LIST_GROUP : slots.stop // LIST_GROUP]
                nc.vector.tensor_copy(gathered[:, slots], pool_tile[:].bitcast(U32).indirect(entries))
            return gathered

        def score(bank, words, plane, t, slots):
            queries = slice(t * P, (t + 1) * P)
            scores = psum.tile([P, slots.stop - slots.start], F32, name="bank", tag="bank%d" % bank)
            nc.tensor.matmul_mx(
                out=scores[:],
                lhsT=q_codes[:, queries].bitcast(FP8X4),
                lhsT_scale=q_scales[:, queries],
                rhs=words[:, slots].bitcast(FP8X4),
                rhs_scale=plane[:, slots],
                start=True,
                stop=True,
            )
            return scores

        gated = keep.tile([P, Q_TILES, SLOTS], F32, name="gated")
        k_got = gather_words(k_pool, "staging")

        a_passes = [(0, 0, 0, P), (1, 1, 0, HALF), (2, 0, P, HALF), (3, 0, HALF, SLOTS), (0, 1, HALF, SLOTS)]
        for bank, t, lo, hi in a_passes:
            a_scores = score(bank, k_got, ks_plane, t, slice(lo, hi))
            nc.scalar.activation(gated[:, t, lo:hi], a_scores[:], silu)

        c_got = gather_words(c_pool, "c_got")
        out_view = out[0].rearrange("(t p) n -> p t n", p=P)
        result = keep.tile([P, Q_TILES, SLOTS], F32, name="result")
        z_passes = [(t, lo) for half in (first, second) for t in range(Q_TILES) for lo in (half.start, half.start + P)]
        z_banks = [4, 2, 1, 3, 5, 7, 0, 6]
        for bank, (t, lo) in zip(z_banks, z_passes):
            slots = slice(lo, lo + P)
            z_scores = score(bank, c_got, cs_plane, t, slots)
            nc.vector.tensor_tensor(result[:, t, slots], z_scores[:], gated[:, t, slots], add)
            if t == 0 and lo < HALF:
                nc.sync.dma_start(out=out_view[:, t, slots], in_=result[:, t, slots])
            elif slots.stop % HALF == 0:
                done = slice(slots.stop - HALF, slots.stop)
                nc.sync.dma_start(out=out_view[:, t, done], in_=result[:, t, done])
